import numpy as np
import ml_dtypes


def mxq(x, axis, fmt="e4m3"):
    dtype, down = {"e4m3": (ml_dtypes.float8_e4m3fn, 7), "e5m2": (ml_dtypes.float8_e5m2, 14)}[fmt]
    v = np.moveaxis(np.asarray(x, np.float32).astype(ml_dtypes.bfloat16).astype(np.float64), axis, -1)
    blocks = v.reshape(v.shape[:-1] + (-1, 32))
    amax = np.abs(blocks).max(-1, keepdims=True)
    byte = np.maximum(np.where(amax > 0, np.frexp(amax)[1] - 1 + 127, 0) - down, 1)
    scale = np.exp2(byte - 127.0)
    codes = (blocks / scale).astype(np.float32).astype(dtype).astype(np.float64)
    return np.moveaxis((codes * scale).reshape(v.shape), -1, axis)


WIDE = False


def mx_kscale(k):
    if not WIDE:
        return np.ones(k)
    levels = np.array([10, -10, 5, -5, 0])
    if k % 512:
        return np.exp2(np.random.permutation(np.resize(levels, k // 32))).repeat(32)
    a = np.empty((k // 512, 16))
    for p in range(k // 512):
        a[p, :8] = np.random.permutation(np.resize(levels, 8))
        for g in range(8):
            far = levels[np.abs(levels - a[p, g]) >= 10]
            a[p, g + 8] = far[np.random.randint(len(far))]
    return np.exp2(a.ravel()).repeat(32)


BF16 = ml_dtypes.bfloat16


def bf(x):
    return np.asarray(x, np.float32).astype(BF16)


def f64(x):
    return np.asarray(x).astype(np.float64)


B, N, D, L = 1, 1024, 512, 512


def centred_beliefs(u, gl):
    p = np.exp(u - u.max(axis=-1, keepdims=True))
    p = p / p.sum(axis=-1, keepdims=True)
    return (L * p - 1.0) * gl[None, None, :]


def signed_affinity(a, e, kg):
    s = (mxq(a, 2, "e4m3") @ mxq(e, 2, "e4m3").transpose(0, 2, 1)) / np.sqrt(D)
    return np.tanh(s) * kg[:, None, :]


def draw0():
    s = mx_kscale(D)
    c = mx_kscale(L)
    r = mx_kscale(N)
    return {"a": bf(np.random.standard_normal((B, N, D)) * s),
            "e": bf(np.random.standard_normal((B, N, D)) / s),
            "u": bf(np.random.standard_normal((B, N, L))),
            "gl": bf((1.0 + 0.1 * np.random.standard_normal(L)) * c),
            "mu": bf(np.random.standard_normal((L, L)) / np.sqrt(L) / c[:, None]),
            "t": bf((1.0 + 0.1 * np.random.standard_normal((B, N))) / r[None, :]),
            "kg": bf((1.0 + 0.1 * np.random.standard_normal((B, N))) * r[None, :])}


def core(a, e, u, gl, mu, t, kg):
    a, e, u, gl, mu, t, kg = f64(a), f64(e), f64(u), f64(gl), f64(mu), f64(t), f64(kg)
    q = centred_beliefs(u, gl)
    v = t[:, :, None] * (mxq(q, 2, "e4m3") @ mxq(mu, 0, "e4m3"))
    kk = signed_affinity(a, e, kg)
    msg = (mxq(kk, 2, "e4m3") @ mxq(v, 1, "e4m3")) / np.sqrt(N)
    return u - msg


def e4m3fn_bytes(y):
    return np.clip(np.asarray(y, np.float64), -448.0, 448.0).astype(np.float32).astype(ml_dtypes.float8_e4m3fn).view(np.uint8)


def e4m3fn_values(b):
    return np.asarray(b, np.uint8).view(ml_dtypes.float8_e4m3fn).astype(np.float64)


def setup_inputs():
    d = draw0()
    x0 = np.asarray(d['e']).astype(np.float64)
    s = (np.max(np.abs(x0), axis=(0, 1), keepdims=True) / 448.0).astype(np.float32)
    out = {}
    for k, v in d.items():
        if k == 'e':
            out['e_bytes'] = e4m3fn_bytes(x0 / s.astype(np.float64))
            out['e_scale'] = s
        else:
            out[k] = v
    return out


def reference(a, e_bytes, e_scale, u, gl, mu, t, kg):
    return core(a, e4m3fn_values(e_bytes) * e_scale.astype(np.float64), u, gl, mu, t, kg)

@@ -1,0 +1,349 @@
+from contextlib import ExitStack
+
+import concourse.mybir as mybir
+from concourse.masks import make_identity
+
+N, D, L = 1024, 512, 512
+FLOPS = 2 * (N * L * L + N * N * D + N * N * L)
+
+F32 = mybir.dt.float32
+BF16 = mybir.dt.bfloat16
+U32 = mybir.dt.uint32
+U8 = mybir.dt.uint8
+FP8 = mybir.dt.float8_e4m3fn
+FP8X4 = mybir.dt.float8_e4m3fn_x4
+ALU = mybir.AluOpType
+ACT = mybir.ActivationFunctionType
+
+P = 128
+G = 2
+T = 4
+S = G * T
+PAIRS = S // 2
+
+
+def tile_signedaffinitymeanfieldstep_kernel(tc, a, e_bytes, e_scale, u, gl, mu, t, kg, out):
+    nc = tc.nc
+    with ExitStack() as ctx:
+        keep = ctx.enter_context(tc.tile_pool(name="keep", bufs=1))
+        work = ctx.enter_context(tc.tile_pool(name="work", bufs=5))
+        psum = ctx.enter_context(tc.psum_pool(name="psum", bufs=1))
+        ctx.enter_context(tc.manual_schedule())
+
+        def rows(x):
+            return x.rearrange("b (g m t) c -> (b g) m t c", g=G, t=T)
+
+        a_v, e_v, u_v, out_v = rows(a), rows(e_bytes), rows(u), rows(out)
+
+        esc = keep.tile([P, T], F32, name="esc")
+        nc.sync.dma_start(out=esc[:], in_=e_scale.rearrange("a b (p j) -> p (a b j)", j=T))
+        u_sb = [keep.tile([P, 2, L], BF16, name=f"u{h}") for h in range(PAIRS)]
+        a_sb = [keep.tile([P, 2, D], BF16, name=f"a{h}") for h in range(PAIRS)]
+        e8 = [keep.tile([P, T, D], U8, name=f"e8_{g}") for g in range(G)]
+        mu_raw = keep.tile([P, T, L], BF16, name="mu_raw")
+        gl_sb = keep.tile([P, T], BF16, name="gl_sb")
+        kg_sb = keep.tile([P, G, T], BF16, name="kg_sb")
+        t_sb = keep.tile([P, G, T], BF16, name="t_sb")
+
+        def load_pair(dst, view, h):
+            nc.sync.dma_start(out=dst[h][:], in_=view[h // 2][:, 2 * (h % 2) : 2 * (h % 2) + 2, :])
+
+        load_pair(u_sb, u_v, 0)
+        nc.sync.dma_start(out=e8[0][:], in_=e_v[0])
+        load_pair(u_sb, u_v, 1)
+        nc.sync.dma_start(out=e8[1][:], in_=e_v[1])
+        load_pair(u_sb, u_v, 2)
+        load_pair(u_sb, u_v, 3)
+        nc.sync.dma_start(out=gl_sb[:], in_=gl.rearrange("(p t) -> p t", t=T))
+        nc.sync.dma_start(out=mu_raw[:], in_=mu.rearrange("(p t) n -> p t n", t=T))
+        nc.sync.dma_start(out=t_sb[:], in_=t.rearrange("b (g p t) -> p (b g) t", g=G, t=T))
+        nc.sync.dma_start(out=kg_sb[:], in_=kg.rearrange("b (g p t) -> p (b g) t", g=G, t=T))
+        for h in range(PAIRS):
+            load_pair(a_sb, a_v, h)
+
+        ident = keep.tile([P, P], F32, name="ident")
+        make_identity(nc, ident[:])
+        warm = keep.tile([P, 1], F32, name="warm")
+        nc.vector.memset(warm[:], 0.0)
+        nc.scalar.activation(out=warm[:], in_=warm[:], func=ACT.Exp)
+
+        neg_max = keep.tile([P, S], F32, name="neg_max")
+        ex_sum = keep.tile([P, S], F32, name="ex_sum")
+        recip = keep.tile([P, S], F32, name="recip")
+        sc_bc = keep.tile([P, D], F32, name="sc_bc")
+        e_bf = [keep.tile([P, D], BF16, name=f"ebf{s}") for s in range(S)]
+        e_grp = [keep.tile([P, T, P, 4], BF16, name=f"egrp{g}", align_bytes=64) for g in range(G)]
+        a_grp = [keep.tile([P, 2, P, 4], BF16, name=f"agrp{h}", align_bytes=64) for h in range(PAIRS)]
+        q_grp = [keep.tile([P, T, P, 4], BF16, name=f"qgrp{g}", align_bytes=64) for g in range(G)]
+        v_grp = [keep.tile([P, L, 4], BF16, name=f"vgrp{g}", align_bytes=64) for g in range(G)]
+        mu_grp = keep.tile([P, L, 4], BF16, name="mu_grp", align_bytes=64)
+
+        def codes(name, width):
+            c = keep.tile([P, width], U32, name=name + "_c", align_bytes=64)
+            p = keep.tile([P, width], U8, name=name + "_s", align_bytes=64)
+            return c, p
+
+        e_q = [codes(f"eq{g}", 512) for g in range(G)]
+        a_q = [codes(f"aq{h}", 256) for h in range(PAIRS)]
+        q_q = [codes(f"qq{g}", 512) for g in range(G)]
+        v_q = [codes(f"vq{g}", 512) for g in range(G)]
+        mu_q = codes("muq", 512)
+
+        def quantize(dst, src):
+            nc.vector.quantize_mx(out=dst[0][:].bitcast(FP8X4), scales=dst[1][:], in_=src)
+
+        def matmul(o, lhs, lc, rhs, rc, start=True, stop=True):
+            nc.tensor.matmul_mx(
+                out=o, lhsT=lhs[0][:, lc].bitcast(FP8X4), lhsT_scale=lhs[1][:, lc],
+                rhs=rhs[0][:, rc].bitcast(FP8X4), rhs_scale=rhs[1][:, rc], start=start, stop=stop)
+
+        bank_no = [0]
+
+        def bank():
+            b = psum.tile([P, 512], F32, name=f"bank{bank_no[0] % 7}")
+            bank_no[0] += 1
+            return b
+
+        banks = {}
+        kg_ps = psum.tile([P, G, T], F32, name="kg_ps")
+        ident_bf = keep.tile([P, P], BF16, name="ident_bf")
+        make_identity(nc, ident_bf[:])
+
+        def kg_t():
+            nc.tensor.matmul(out=kg_ps[:].rearrange("p g t -> p (g t)"), lhsT=ident_bf[:], rhs=kg_sb[:].rearrange("p g t -> p (g t)"), start=True, stop=True)
+
+        def scale_t():
+            b = bank()
+            for j in range(T):
+                nc.tensor.transpose(b[:, j * P : (j + 1) * P], esc[:, j : j + 1].to_broadcast([P, P]), ident[:])
+            nc.scalar.copy(out=sc_bc[:].rearrange("p (q j) -> p q j", j=T), in_=b[:].rearrange("p (j q) -> p q j", j=T))
+
+        def e_mul(s):
+            nc.vector.tensor_tensor(out=e_bf[s][:], in0=e8[s // T][:, s % T, :].bitcast(FP8), in1=sc_bc[:], op=ALU.mult)
+
+        def word_t(key, srcs):
+            b = bank()
+            for i, src in enumerate(srcs):
+                w = src.bitcast(F32)
+                for k in range(2):
+                    nc.tensor.transpose(b[:, (2 * i + k) * P : (2 * i + k + 1) * P], w[:, k : 256 : 2], ident[:])
+            banks[key] = b
+
+        def word_copy(key, dst):
+            nc.scalar.copy(out=dst.bitcast(F32), in_=banks[key][:].rearrange("p (s k r) -> p s r k", s=2, k=2))
+
+        def e_t(h):
+            word_t(("e", h), [e_bf[2 * h][:], e_bf[2 * h + 1][:]])
+
+        def e_c(h):
+            word_copy(("e", h), e_grp[h // 2][:, 2 * (h % 2) : 2 * (h % 2) + 2, :, :])
+
+        def a_t(h):
+            word_t(("a", h), [a_sb[h][:, 0, :], a_sb[h][:, 1, :]])
+
+        def a_c(h):
+            word_copy(("a", h), a_grp[h][:])
+
+        def row_max(s):
+            dump = work.tile([P, L], BF16, name="dump")
+            nc.vector.tensor_scalar(out=dump[:], in0=u_sb[s // 2][:, s % 2, :], scalar1=-1.0, scalar2=None,
+                                    op0=ALU.mult, op1=ALU.min, accum_out=neg_max[:, s : s + 1])
+
+        def exp(s):
+            x = work.tile([P, T, P], F32, name="ex")
+            nc.scalar.activation(out=x[:], in_=u_sb[s // 2][:, s % 2, :].rearrange("m (p t) -> m t p", t=T),
+                                 func=ACT.Exp, bias=neg_max[:, s : s + 1], accum_out=ex_sum[:, s : s + 1])
+            banks[("ex", s)] = x
+
+        def rec(h):
+            nc.vector.reciprocal(out=recip[:, 2 * h : 2 * h + 2], in_=ex_sum[:, 2 * h : 2 * h + 2])
+
+        def z(s):
+            zz = work.tile([P, T, P], F32, name="z")
+            nc.gpsimd.tensor_scalar(out=zz[:], in0=banks[("ex", s)][:], scalar1=recip[:, s : s + 1], scalar2=-1.0 / L, op0=ALU.mult, op1=ALU.add)
+            banks[("z", s)] = zz
+
+        def z_t(s):
+            b = bank()
+            for j in range(T):
+                nc.tensor.transpose(b[:, j * P : (j + 1) * P], banks[("z", s)][:, j, :], ident[:])
+            banks[("zt", s)] = b
+
+        def per_word(v):
+            return v.unsqueeze(1).to_broadcast([P, P, T])
+
+        def q_mul(s):
+            nc.vector.tensor_tensor(out=q_grp[s // T][:, s % T, :, :],
+                                    in0=banks[("zt", s)][:].rearrange("p (t m) -> p m t", t=T),
+                                    in1=per_word(gl_sb[:]), op=ALU.mult)
+
+        def v_mm(g, lb):
+            b = bank()
+            for j in range(T):
+                matmul(b[:, j * P : (j + 1) * P], q_q[g], slice(j * P, (j + 1) * P), mu_q, slice(lb * P, (lb + 1) * P))
+            banks[("v", g, lb)] = b
+
+        def v_mul(g, lb):
+            nc.vector.tensor_tensor(out=v_grp[g][:, lb * P : (lb + 1) * P, :],
+                                    in0=banks[("v", g, lb)][:].rearrange("p (t m) -> p m t", t=T),
+                                    in1=per_word(t_sb[:, g, :]), op=ALU.mult)
+
+        def s_mm(g, ib):
+            b = bank()
+            c = slice((ib % 2) * P, (ib % 2 + 1) * P)
+            for j in range(T):
+                matmul(b[:, j * P : (j + 1) * P], e_q[g], slice(j * P, (j + 1) * P), a_q[ib // 2], c)
+            banks[("s", g, ib)] = b
+
+        def tanh(g, ib):
+            if ("th", ib) not in banks:
+                x = work.tile([P, G, P, T], F32, name="th")
+                banks[("th", ib)] = x
+            nc.scalar.activation(out=banks[("th", ib)][:, g, :, :], in_=banks[("s", g, ib)][:].rearrange("p (t m) -> p m t", t=T),
+                                 func=ACT.Tanh, scale=D ** -0.5)
+
+        def kk(ib):
+            if ("kk", ib) not in banks:
+                x = work.tile([P, G, P, T], BF16, name="kk", align_bytes=64)
+                banks[("kk", ib)] = x
+            return banks[("kk", ib)]
+
+        def k_mul(g, ib):
+            nc.vector.tensor_tensor(out=kk(ib)[:, g, :, :], in0=banks[("th", ib)][:, g, :, :],
+                                    in1=per_word(kg_ps[:, g, :]), op=ALU.mult)
+
+        def k_mul_g(g, ib):
+            nc.gpsimd.tensor_tensor(out=kk(ib)[:, g, :, :], in0=banks[("th", ib)][:, g, :, :],
+                                    in1=per_word(kg_sb[:, g, :]), op=ALU.mult)
+
+        def k_quant(ib):
+            c = work.tile([P, G * P], U32, name="kc", align_bytes=64)
+            p = work.tile([P, G * P], U8, name="ks", align_bytes=64)
+            banks[("kq", ib)] = (c, p)
+            quantize((c, p), banks[("kk", ib)][:].rearrange("p g m t -> p (g m t)"))
+
+        def o_mm(ib):
+            b = bank()
+            for g in range(G):
+                matmul(b[:], banks[("kq", ib)], slice(g * P, (g + 1) * P), v_q[g], slice(0, L), start=(g == 0), stop=(g == G - 1))
+            banks[("o", ib)] = b
+
+        def finish(ib):
+            o = work.tile([P, L], F32, name="o")
+            nc.vector.scalar_tensor_tensor(out=o[:], in0=banks[("o", ib)][:], scalar=-float(L) * N ** -0.5,
+                                           in1=u_sb[ib // 2][:, ib % 2, :], op0=ALU.mult, op1=ALU.add)
+            nc.sync.dma_start(out=out_v[ib // T][:, ib % T, :], in_=o[:])
+
+        def each(f, *xs):
+            for x in xs:
+                f(x)
+
+        scale_t()
+        kg_t()
+        each(row_max, 0, 1)
+        each(exp, 0, 1)
+        each(e_mul, 0, 1)
+        each(row_max, 2, 3)
+        e_t(0)
+        each(exp, 2, 3)
+        each(e_mul, 2, 3)
+        rec(0)
+        each(z, 0, 1)
+        e_c(0)
+        e_t(1)
+        each(row_max, 4, 5)
+        rec(1)
+        each(exp, 4, 5)
+        each(z, 2, 3)
+        e_c(1)
+        each(e_mul, 4, 5)
+        each(z_t, 0, 1)
+        each(z_t, 2, 3)
+        each(row_max, 6, 7)
+        rec(2)
+        each(exp, 6, 7)
+        e_t(2)
+        each(q_mul, 0, 1)
+        quantize(e_q[0], e_grp[0][:].rearrange("p t m w -> p (t m w)"))
+        each(z, 4, 5)
+        each(q_mul, 2, 3)
+        rec(3)
+        e_c(2)
+        nc.scalar.copy(out=mu_grp[:, 0:256, :], in_=mu_raw[:, :, 0:256].rearrange("p t n -> p n t"))
+        nc.scalar.copy(out=mu_grp[:, 256:512, :], in_=mu_raw[:, :, 256:512].rearrange("p t n -> p n t"))
+        each(z_t, 4, 5)
+        quantize(q_q[0], q_grp[0][:].rearrange("p t m w -> p (t m w)"))
+        each(e_mul, 6, 7)
+        each(z, 6, 7)
+        e_t(3)
+        each(q_mul, 4, 5)
+        e_c(3)
+        each(z_t, 6, 7)
+        quantize(mu_q, mu_grp[:].rearrange("p n t -> p (n t)"))
+        v_mm(0, 0)
+        v_mm(0, 1)
+        each(q_mul, 6, 7)
+        a_t(0)
+        a_c(0)
+        quantize(e_q[1], e_grp[1][:].rearrange("p t m w -> p (t m w)"))
+        v_mul(0, 0)
+        v_mm(0, 2)
+        v_mul(0, 1)
+        v_mm(0, 3)
+        a_t(1)
+        a_c(1)
+        quantize(q_q[1], q_grp[1][:].rearrange("p t m w -> p (t m w)"))
+        quantize(a_q[0], a_grp[0][:].rearrange("p t m w -> p (t m w)"))
+        s_mm(1, 0)
+        s_mm(0, 0)
+        tanh(1, 0)
+        tanh(0, 0)
+        v_mul(0, 2)
+        quantize(a_q[1], a_grp[1][:].rearrange("p t m w -> p (t m w)"))
+        v_mul(0, 3)
+        v_mm(1, 0)
+        v_mm(1, 1)
+        k_mul_g(1, 0)
+        a_t(2)
+        a_c(2)
+        s_mm(1, 1)
+        s_mm(0, 1)
+        tanh(1, 1)
+        tanh(0, 1)
+        v_mul(1, 0)
+        v_mul(1, 1)
+        v_mm(1, 2)
+        v_mm(1, 3)
+        a_t(3)
+        a_c(3)
+        quantize(v_q[0], v_grp[0][:].rearrange("p n t -> p (n t)"))
+        v_mul(1, 2)
+        k_mul_g(1, 1)
+        v_mul(1, 3)
+        s_mm(1, 2)
+        s_mm(0, 2)
+        tanh(1, 2)
+        tanh(0, 2)
+        quantize(a_q[2], a_grp[2][:].rearrange("p t m w -> p (t m w)"))
+        quantize(v_q[1], v_grp[1][:].rearrange("p n t -> p (n t)"))
+        quantize(a_q[3], a_grp[3][:].rearrange("p t m w -> p (t m w)"))
+        k_mul(0, 0)
+        s_mm(1, 3)
+        s_mm(0, 3)
+        tanh(1, 3)
+        tanh(0, 3)
+        for ib in range(S):
+            k_quant(ib)
+            o_mm(ib)
+            if ib + 2 < S:
+                k_mul_g(1, ib + 2)
+            if ib + 4 < S:
+                s_mm(1, ib + 4)
+                s_mm(0, ib + 4)
+                tanh(1, ib + 4)
+                tanh(0, ib + 4)
+            if ib + 1 < S:
+                k_mul(0, ib + 1)
+            if ib > 0:
+                finish(ib - 1)
+        finish(S - 1)

@@ -26,7 +26,7 @@ def tile_signedaffinitymeanfieldstep_kernel(tc, a, e_bytes, e_scale, u, gl, mu, 
     nc = tc.nc
     with ExitStack() as ctx:
         keep = ctx.enter_context(tc.tile_pool(name="keep", bufs=1))
-        work = ctx.enter_context(tc.tile_pool(name="work", bufs=5))
+        work = ctx.enter_context(tc.tile_pool(name="work", bufs=8))
         psum = ctx.enter_context(tc.psum_pool(name="psum", bufs=1))
         ctx.enter_context(tc.manual_schedule())
 
@@ -54,10 +54,10 @@ def tile_signedaffinitymeanfieldstep_kernel(tc, a, e_bytes, e_scale, u, gl, mu, 
         nc.sync.dma_start(out=e8[1][:], in_=e_v[1])
         load_pair(u_sb, u_v, 2)
         load_pair(u_sb, u_v, 3)
+        nc.sync.dma_start(out=kg_sb[:], in_=kg.rearrange("b (g p t) -> p (b g) t", g=G, t=T))
         nc.sync.dma_start(out=gl_sb[:], in_=gl.rearrange("(p t) -> p t", t=T))
         nc.sync.dma_start(out=mu_raw[:], in_=mu.rearrange("(p t) n -> p t n", t=T))
         nc.sync.dma_start(out=t_sb[:], in_=t.rearrange("b (g p t) -> p (b g) t", g=G, t=T))
-        nc.sync.dma_start(out=kg_sb[:], in_=kg.rearrange("b (g p t) -> p (b g) t", g=G, t=T))
         for h in range(PAIRS):
             load_pair(a_sb, a_v, h)
 
@@ -116,7 +116,10 @@ def tile_signedaffinitymeanfieldstep_kernel(tc, a, e_bytes, e_scale, u, gl, mu, 
             b = bank()
             for j in range(T):
                 nc.tensor.transpose(b[:, j * P : (j + 1) * P], esc[:, j : j + 1].to_broadcast([P, P]), ident[:])
-            nc.scalar.copy(out=sc_bc[:].rearrange("p (q j) -> p q j", j=T), in_=b[:].rearrange("p (j q) -> p q j", j=T))
+            banks["sc"] = b
+
+        def scale_c():
+            nc.scalar.copy(out=sc_bc[:].rearrange("p (q j) -> p q j", j=T), in_=banks["sc"][:].rearrange("p (j q) -> p q j", j=T))
 
         def e_mul(s):
             nc.vector.tensor_tensor(out=e_bf[s][:], in0=e8[s // T][:, s % T, :].bitcast(FP8), in1=sc_bc[:], op=ALU.mult)
@@ -158,9 +161,14 @@ def tile_signedaffinitymeanfieldstep_kernel(tc, a, e_bytes, e_scale, u, gl, mu, 
         def rec(h):
             nc.vector.reciprocal(out=recip[:, 2 * h : 2 * h + 2], in_=ex_sum[:, 2 * h : 2 * h + 2])
 
-        def z(s):
+        def z(s, eng):
             zz = work.tile([P, T, P], F32, name="z")
-            nc.gpsimd.tensor_scalar(out=zz[:], in0=banks[("ex", s)][:], scalar1=recip[:, s : s + 1], scalar2=-1.0 / L, op0=ALU.mult, op1=ALU.add)
+            if eng == "S":
+                nc.scalar.activation(out=zz[:], in_=banks[("ex", s)][:], func=ACT.Identity, scale=recip[:, s : s + 1], bias=-1.0 / L)
+            elif eng == "V":
+                nc.vector.tensor_scalar(out=zz[:], in0=banks[("ex", s)][:], scalar1=recip[:, s : s + 1], scalar2=-1.0 / L, op0=ALU.mult, op1=ALU.add)
+            else:
+                nc.gpsimd.tensor_scalar(out=zz[:], in0=banks[("ex", s)][:], scalar1=recip[:, s : s + 1], scalar2=-1.0 / L, op0=ALU.mult, op1=ALU.add)
             banks[("z", s)] = zz
 
         def z_t(s):
@@ -171,6 +179,29 @@ def tile_signedaffinitymeanfieldstep_kernel(tc, a, e_bytes, e_scale, u, gl, mu, 
 
         def per_word(v):
             return v.unsqueeze(1).to_broadcast([P, P, T])
+
+        def q_mul_s(s):
+            for j in range(T):
+                nc.scalar.activation(out=q_grp[s // T][:, s % T, :, j], in_=banks[("zt", s)][:, j * P : (j + 1) * P],
+                                     func=ACT.Copy, scale=gl_f[:, j : j + 1])
+
+        def v_mul_s(g, lb):
+            for j in range(T):
+                nc.scalar.activation(out=v_grp[g][:, lb * P : (lb + 1) * P, j], in_=banks[("v", g, lb)][:, j * P : (j + 1) * P],
+                                     func=ACT.Copy, scale=t_f[:, g, j : j + 1])
+
+        gl_f = keep.tile([P, T], F32, name="gl_f")
+        nc.gpsimd.tensor_copy(out=gl_f[:], in_=gl_sb[:])
+        t_f = keep.tile([P, G, T], F32, name="t_f")
+        nc.gpsimd.tensor_copy(out=t_f[:], in_=t_sb[:])
+
+        def mu_copy(h, eng):
+            c = slice(256 * h, 256 * h + 256)
+            dst, src = mu_grp[:, c, :], mu_raw[:, :, c].rearrange("p t n -> p n t")
+            if eng == "S":
+                nc.scalar.copy(out=dst, in_=src)
+            else:
+                nc.vector.tensor_copy(out=dst, in_=src)
 
         def q_mul(s):
             nc.vector.tensor_tensor(out=q_grp[s // T][:, s % T, :, :],
@@ -238,112 +269,175 @@ def tile_signedaffinitymeanfieldstep_kernel(tc, a, e_bytes, e_scale, u, gl, mu, 
             for x in xs:
                 f(x)
 
+        row_max(0)
+        row_max(1)
         scale_t()
-        kg_t()
-        each(row_max, 0, 1)
-        each(exp, 0, 1)
-        each(e_mul, 0, 1)
-        each(row_max, 2, 3)
+        scale_c()
+        e_mul(0)
+        e_mul(1)
         e_t(0)
-        each(exp, 2, 3)
-        each(e_mul, 2, 3)
+        e_mul(2)
+        exp(1)
+        e_mul(3)
+        row_max(6)
+        exp(0)
         rec(0)
-        each(z, 0, 1)
         e_c(0)
+        exp(6)
+        row_max(5)
+        row_max(4)
+        row_max(3)
+        row_max(7)
+        exp(4)
+        exp(7)
+        mu_copy(1, "V")
         e_t(1)
-        each(row_max, 4, 5)
-        rec(1)
-        each(exp, 4, 5)
-        each(z, 2, 3)
-        e_c(1)
-        each(e_mul, 4, 5)
-        each(z_t, 0, 1)
-        each(z_t, 2, 3)
-        each(row_max, 6, 7)
-        rec(2)
-        each(exp, 6, 7)
-        e_t(2)
-        each(q_mul, 0, 1)
-        quantize(e_q[0], e_grp[0][:].rearrange("p t m w -> p (t m w)"))
-        each(z, 4, 5)
-        each(q_mul, 2, 3)
-        rec(3)
-        e_c(2)
-        nc.scalar.copy(out=mu_grp[:, 0:256, :], in_=mu_raw[:, :, 0:256].rearrange("p t n -> p n t"))
-        nc.scalar.copy(out=mu_grp[:, 256:512, :], in_=mu_raw[:, :, 256:512].rearrange("p t n -> p n t"))
-        each(z_t, 4, 5)
-        quantize(q_q[0], q_grp[0][:].rearrange("p t m w -> p (t m w)"))
-        each(e_mul, 6, 7)
-        each(z, 6, 7)
-        e_t(3)
-        each(q_mul, 4, 5)
-        e_c(3)
-        each(z_t, 6, 7)
-        quantize(mu_q, mu_grp[:].rearrange("p n t -> p (n t)"))
-        v_mm(0, 0)
-        v_mm(0, 1)
-        each(q_mul, 6, 7)
+        e_mul(5)
         a_t(0)
-        a_c(0)
-        quantize(e_q[1], e_grp[1][:].rearrange("p t m w -> p (t m w)"))
-        v_mul(0, 0)
-        v_mm(0, 2)
-        v_mul(0, 1)
-        v_mm(0, 3)
         a_t(1)
-        a_c(1)
-        quantize(q_q[1], q_grp[1][:].rearrange("p t m w -> p (t m w)"))
+        exp(5)
+        e_mul(6)
+        a_c(0)
+        exp(3)
+        rec(3)
+        e_mul(7)
+        e_mul(4)
         quantize(a_q[0], a_grp[0][:].rearrange("p t m w -> p (t m w)"))
-        s_mm(1, 0)
-        s_mm(0, 0)
-        tanh(1, 0)
-        tanh(0, 0)
-        v_mul(0, 2)
+        row_max(2)
+        a_t(2)
+        e_c(1)
+        e_t(3)
+        rec(2)
+        quantize(e_q[0], e_grp[0][:].rearrange("p t m w -> p (t m w)"))
+        z(1, "G")
+        a_c(1)
+        z(0, "G")
         quantize(a_q[1], a_grp[1][:].rearrange("p t m w -> p (t m w)"))
-        v_mul(0, 3)
+        e_t(2)
+        s_mm(0, 0)
+        s_mm(0, 3)
+        exp(2)
+        mu_copy(0, "V")
+        a_c(2)
+        e_c(3)
+        z(6, "S")
+        e_c(2)
+        rec(1)
+        tanh(0, 0)
+        quantize(a_q[2], a_grp[2][:].rearrange("p t m w -> p (t m w)"))
+        z(7, "G")
+        z(5, "V")
+        z_t(7)
+        z_t(6)
+        kg_t()
+        quantize(mu_q, mu_grp[:].rearrange("p n t -> p (n t)"))
+        s_mm(0, 1)
+        tanh(0, 3)
+        s_mm(0, 2)
+        z_t(0)
+        z(4, "S")
+        tanh(0, 2)
+        z(3, "S")
+        quantize(e_q[1], e_grp[1][:].rearrange("p t m w -> p (t m w)"))
+        z_t(4)
+        z_t(5)
+        tanh(0, 1)
+        a_t(3)
+        q_mul(7)
+        z(2, "G")
+        s_mm(1, 0)
+        s_mm(1, 3)
+        q_mul(6)
+        a_c(3)
+        q_mul(0)
+        q_mul(4)
+        s_mm(1, 1)
+        q_mul(5)
+        tanh(1, 0)
+        tanh(1, 3)
+        quantize(q_q[1], q_grp[1][:].rearrange("p t m w -> p (t m w)"))
+        z_t(1)
+        k_mul_g(0, 0)
+        quantize(a_q[3], a_grp[3][:].rearrange("p t m w -> p (t m w)"))
+        z_t(2)
+        k_mul(0, 3)
+        z_t(3)
+        s_mm(1, 2)
+        s_mm(1, 7)
+        q_mul(1)
+        tanh(1, 1)
+        q_mul(2)
+        tanh(1, 7)
+        q_mul(3)
+        s_mm(0, 6)
+        quantize(q_q[0], q_grp[0][:].rearrange("p t m w -> p (t m w)"))
+        s_mm(0, 5)
+        k_mul(0, 1)
+        k_mul(1, 3)
+        s_mm(1, 5)
+        v_mm(0, 2)
+        tanh(1, 2)
+        k_mul_g(0, 2)
+        tanh(0, 6)
+        v_mm(0, 0)
+        tanh(0, 5)
+        v_mul(0, 2)
+        v_mm(0, 1)
+        v_mul(0, 1)
+        v_mm(1, 2)
+        s_mm(0, 7)
+        v_mul(0, 0)
         v_mm(1, 0)
+        k_mul(1, 2)
+        tanh(1, 5)
+        v_mm(0, 3)
+        tanh(0, 7)
         v_mm(1, 1)
         k_mul_g(1, 0)
-        a_t(2)
-        a_c(2)
-        s_mm(1, 1)
-        s_mm(0, 1)
-        tanh(1, 1)
-        tanh(0, 1)
         v_mul(1, 0)
-        v_mul(1, 1)
-        v_mm(1, 2)
         v_mm(1, 3)
-        a_t(3)
-        a_c(3)
-        quantize(v_q[0], v_grp[0][:].rearrange("p n t -> p (n t)"))
-        v_mul(1, 2)
+        v_mul(0, 3)
         k_mul_g(1, 1)
+        v_mul(1, 1)
+        k_mul_g(1, 7)
         v_mul(1, 3)
-        s_mm(1, 2)
-        s_mm(0, 2)
-        tanh(1, 2)
-        tanh(0, 2)
-        quantize(a_q[2], a_grp[2][:].rearrange("p t m w -> p (t m w)"))
+        v_mul(1, 2)
+        k_quant(0)
         quantize(v_q[1], v_grp[1][:].rearrange("p n t -> p (n t)"))
-        quantize(a_q[3], a_grp[3][:].rearrange("p t m w -> p (t m w)"))
-        k_mul(0, 0)
-        s_mm(1, 3)
-        s_mm(0, 3)
-        tanh(1, 3)
-        tanh(0, 3)
-        for ib in range(S):
-            k_quant(ib)
-            o_mm(ib)
-            if ib + 2 < S:
-                k_mul_g(1, ib + 2)
-            if ib + 4 < S:
-                s_mm(1, ib + 4)
-                s_mm(0, ib + 4)
-                tanh(1, ib + 4)
-                tanh(0, ib + 4)
-            if ib + 1 < S:
-                k_mul(0, ib + 1)
-            if ib > 0:
-                finish(ib - 1)
-        finish(S - 1)
+        s_mm(1, 6)
+        quantize(v_q[0], v_grp[0][:].rearrange("p n t -> p (n t)"))
+        k_quant(1)
+        s_mm(0, 4)
+        s_mm(1, 4)
+        tanh(1, 6)
+        tanh(1, 4)
+        o_mm(0)
+        k_quant(3)
+        k_mul_g(0, 6)
+        o_mm(1)
+        k_mul_g(0, 5)
+        k_mul_g(0, 7)
+        k_quant(2)
+        tanh(0, 4)
+        k_mul_g(1, 6)
+        k_quant(7)
+        k_mul_g(1, 4)
+        o_mm(2)
+        k_quant(6)
+        finish(0)
+        finish(1)
+        o_mm(7)
+        k_mul_g(1, 5)
+        finish(2)
+        o_mm(6)
+        k_mul(0, 4)
+        o_mm(3)
+        finish(6)
+        k_quant(5)
+        o_mm(5)
+        k_quant(4)
+        o_mm(4)
+        finish(7)
+        finish(3)
+        finish(5)
+        finish(4)

@@ -270,174 +270,174 @@ def tile_signedaffinitymeanfieldstep_kernel(tc, a, e_bytes, e_scale, u, gl, mu, 
                 f(x)
 
         row_max(0)
-        row_max(1)
         scale_t()
+        row_max(1)
         scale_c()
-        e_mul(0)
-        e_mul(1)
-        e_t(0)
-        e_mul(2)
-        exp(1)
-        e_mul(3)
-        row_max(6)
         exp(0)
-        rec(0)
-        e_c(0)
-        exp(6)
-        row_max(5)
-        row_max(4)
-        row_max(3)
-        row_max(7)
-        exp(4)
-        exp(7)
-        mu_copy(1, "V")
-        e_t(1)
-        e_mul(5)
-        a_t(0)
-        a_t(1)
-        exp(5)
-        e_mul(6)
-        a_c(0)
-        exp(3)
-        rec(3)
-        e_mul(7)
-        e_mul(4)
-        quantize(a_q[0], a_grp[0][:].rearrange("p t m w -> p (t m w)"))
+        e_mul(1)
+        e_mul(0)
+        e_t(0)
+        exp(1)
         row_max(2)
-        a_t(2)
-        e_c(1)
-        e_t(3)
-        rec(2)
-        quantize(e_q[0], e_grp[0][:].rearrange("p t m w -> p (t m w)"))
-        z(1, "G")
-        a_c(1)
-        z(0, "G")
-        quantize(a_q[1], a_grp[1][:].rearrange("p t m w -> p (t m w)"))
-        e_t(2)
-        s_mm(0, 0)
-        s_mm(0, 3)
+        rec(0)
+        e_mul(7)
+        e_mul(6)
+        z(1, "S")
+        z_t(1)
+        z(0, "S")
         exp(2)
+        e_t(3)
+        row_max(6)
+        a_t(0)
+        a_t(2)
+        e_c(0)
+        row_max(7)
+        row_max(3)
+        exp(7)
         mu_copy(0, "V")
-        a_c(2)
+        exp(3)
+        e_mul(4)
         e_c(3)
-        z(6, "S")
-        e_c(2)
+        e_mul(5)
+        e_mul(3)
+        e_t(2)
+        exp(6)
         rec(1)
-        tanh(0, 0)
+        z(2, "S")
+        e_mul(2)
+        z_t(2)
+        mu_copy(1, "V")
+        a_c(2)
+        z(3, "G")
+        row_max(4)
+        a_t(1)
+        e_t(1)
+        q_mul(1)
+        e_c(2)
+        rec(3)
+        a_c(0)
+        exp(4)
+        z_t(3)
+        quantize(e_q[1], e_grp[1][:].rearrange("p t m w -> p (t m w)"))
+        a_c(1)
+        row_max(5)
+        e_c(1)
+        z_t(0)
+        q_mul(2)
+        exp(5)
+        quantize(a_q[0], a_grp[0][:].rearrange("p t m w -> p (t m w)"))
+        quantize(a_q[1], a_grp[1][:].rearrange("p t m w -> p (t m w)"))
         quantize(a_q[2], a_grp[2][:].rearrange("p t m w -> p (t m w)"))
-        z(7, "G")
-        z(5, "V")
-        z_t(7)
-        z_t(6)
-        kg_t()
+        quantize(e_q[0], e_grp[0][:].rearrange("p t m w -> p (t m w)"))
+        rec(2)
+        z(6, "S")
+        q_mul(0)
+        q_mul(3)
+        s_mm(1, 4)
+        s_mm(0, 0)
+        z(4, "S")
+        s_mm(1, 0)
         quantize(mu_q, mu_grp[:].rearrange("p n t -> p (n t)"))
         s_mm(0, 1)
-        tanh(0, 3)
-        s_mm(0, 2)
-        z_t(0)
-        z(4, "S")
-        tanh(0, 2)
-        z(3, "S")
-        quantize(e_q[1], e_grp[1][:].rearrange("p t m w -> p (t m w)"))
+        tanh(1, 4)
         z_t(4)
-        z_t(5)
-        tanh(0, 1)
-        a_t(3)
-        q_mul(7)
-        z(2, "G")
-        s_mm(1, 0)
-        s_mm(1, 3)
-        q_mul(6)
-        a_c(3)
-        q_mul(0)
-        q_mul(4)
-        s_mm(1, 1)
-        q_mul(5)
-        tanh(1, 0)
-        tanh(1, 3)
-        quantize(q_q[1], q_grp[1][:].rearrange("p t m w -> p (t m w)"))
-        z_t(1)
-        k_mul_g(0, 0)
-        quantize(a_q[3], a_grp[3][:].rearrange("p t m w -> p (t m w)"))
-        z_t(2)
-        k_mul(0, 3)
-        z_t(3)
-        s_mm(1, 2)
-        s_mm(1, 7)
-        q_mul(1)
-        tanh(1, 1)
-        q_mul(2)
-        tanh(1, 7)
-        q_mul(3)
-        s_mm(0, 6)
+        z_t(6)
         quantize(q_q[0], q_grp[0][:].rearrange("p t m w -> p (t m w)"))
-        s_mm(0, 5)
-        k_mul(0, 1)
-        k_mul(1, 3)
-        s_mm(1, 5)
-        v_mm(0, 2)
+        kg_t()
+        tanh(0, 0)
+        tanh(1, 0)
+        s_mm(1, 2)
+        k_mul(1, 4)
+        z(5, "S")
+        z(7, "G")
+        tanh(0, 1)
+        s_mm(1, 1)
         tanh(1, 2)
-        k_mul_g(0, 2)
-        tanh(0, 6)
-        v_mm(0, 0)
-        tanh(0, 5)
-        v_mul(0, 2)
-        v_mm(0, 1)
-        v_mul(0, 1)
-        v_mm(1, 2)
-        s_mm(0, 7)
-        v_mul(0, 0)
-        v_mm(1, 0)
-        k_mul(1, 2)
-        tanh(1, 5)
+        q_mul(6)
+        z_t(5)
+        a_t(3)
+        tanh(1, 1)
+        z_t(7)
+        s_mm(0, 2)
+        s_mm(0, 5)
+        s_mm(1, 3)
+        a_c(3)
+        tanh(0, 2)
         v_mm(0, 3)
-        tanh(0, 7)
-        v_mm(1, 1)
-        k_mul_g(1, 0)
-        v_mul(1, 0)
-        v_mm(1, 3)
-        v_mul(0, 3)
-        k_mul_g(1, 1)
-        v_mul(1, 1)
-        k_mul_g(1, 7)
-        v_mul(1, 3)
-        v_mul(1, 2)
+        k_mul_g(0, 0)
+        q_mul(4)
+        tanh(0, 5)
+        tanh(1, 3)
+        s_mm(1, 5)
+        s_mm(0, 4)
+        tanh(1, 5)
+        s_mm(0, 3)
+        k_mul(1, 0)
+        q_mul(5)
+        q_mul(7)
+        quantize(a_q[3], a_grp[3][:].rearrange("p t m w -> p (t m w)"))
+        tanh(0, 4)
+        v_mm(0, 1)
         k_quant(0)
-        quantize(v_q[1], v_grp[1][:].rearrange("p n t -> p (n t)"))
-        s_mm(1, 6)
+        quantize(q_q[1], q_grp[1][:].rearrange("p t m w -> p (t m w)"))
+        v_mul(0, 3)
+        v_mm(1, 3)
+        k_mul_g(0, 1)
+        k_mul(0, 5)
+        v_mm(1, 1)
+        v_mm(1, 0)
+        v_mm(0, 0)
+        v_mm(0, 2)
+        tanh(0, 3)
+        k_mul(1, 1)
+        v_mul(0, 1)
+        s_mm(0, 7)
+        k_mul_g(0, 2)
+        v_mul(1, 0)
+        v_mm(1, 2)
+        k_mul(1, 3)
+        k_mul_g(0, 4)
+        s_mm(0, 6)
+        v_mul(0, 2)
+        k_mul(1, 5)
+        v_mul(0, 0)
+        v_mul_s(1, 1)
+        k_mul(0, 3)
+        v_mul_s(1, 3)
+        k_quant(5)
+        k_quant(3)
+        v_mul_s(1, 2)
+        k_mul_g(1, 2)
+        k_quant(2)
+        tanh(0, 6)
         quantize(v_q[0], v_grp[0][:].rearrange("p n t -> p (n t)"))
         k_quant(1)
-        s_mm(0, 4)
-        s_mm(1, 4)
-        tanh(1, 6)
-        tanh(1, 4)
-        o_mm(0)
-        k_quant(3)
-        k_mul_g(0, 6)
-        o_mm(1)
-        k_mul_g(0, 5)
-        k_mul_g(0, 7)
-        k_quant(2)
-        tanh(0, 4)
-        k_mul_g(1, 6)
-        k_quant(7)
-        k_mul_g(1, 4)
+        s_mm(1, 7)
+        quantize(v_q[1], v_grp[1][:].rearrange("p n t -> p (n t)"))
+        s_mm(1, 6)
         o_mm(2)
-        k_quant(6)
-        finish(0)
-        finish(1)
-        o_mm(7)
-        k_mul_g(1, 5)
-        finish(2)
-        o_mm(6)
-        k_mul(0, 4)
-        o_mm(3)
-        finish(6)
-        k_quant(5)
-        o_mm(5)
+        tanh(0, 7)
         k_quant(4)
+        tanh(1, 7)
+        o_mm(1)
+        o_mm(5)
+        tanh(1, 6)
+        o_mm(3)
+        k_mul(0, 7)
+        k_mul(1, 7)
+        finish(2)
         o_mm(4)
-        finish(7)
-        finish(3)
+        k_mul_g(0, 6)
+        o_mm(0)
+        finish(1)
+        k_mul_g(1, 6)
         finish(5)
+        finish(3)
+        k_quant(7)
         finish(4)
+        o_mm(7)
+        k_quant(6)
+        o_mm(6)
+        finish(0)
+        finish(7)
+        finish(6)

from contextlib import ExitStack

import concourse.mybir as mybir
from concourse.masks import make_identity

N, D, L = 1024, 512, 512
FLOPS = 2 * (N * L * L + N * N * D + N * N * L)

F32 = mybir.dt.float32
BF16 = mybir.dt.bfloat16
U32 = mybir.dt.uint32
U8 = mybir.dt.uint8
FP8 = mybir.dt.float8_e4m3fn
FP8X4 = mybir.dt.float8_e4m3fn_x4
ALU = mybir.AluOpType
ACT = mybir.ActivationFunctionType

P = 128
G = 2
T = 4
S = G * T
PAIRS = S // 2


def tile_signedaffinitymeanfieldstep_kernel(tc, a, e_bytes, e_scale, u, gl, mu, t, kg, out):
    nc = tc.nc
    with ExitStack() as ctx:
        keep = ctx.enter_context(tc.tile_pool(name="keep", bufs=1))
        work = ctx.enter_context(tc.tile_pool(name="work", bufs=8))
        psum = ctx.enter_context(tc.psum_pool(name="psum", bufs=1))
        ctx.enter_context(tc.manual_schedule())

        def rows(x):
            return x.rearrange("b (g m t) c -> (b g) m t c", g=G, t=T)

        a_v, e_v, u_v, out_v = rows(a), rows(e_bytes), rows(u), rows(out)

        esc = keep.tile([P, T], F32, name="esc")
        nc.sync.dma_start(out=esc[:], in_=e_scale.rearrange("a b (p j) -> p (a b j)", j=T))
        u_sb = [keep.tile([P, 2, L], BF16, name=f"u{h}") for h in range(PAIRS)]
        a_sb = [keep.tile([P, 2, D], BF16, name=f"a{h}") for h in range(PAIRS)]
        e8 = [keep.tile([P, T, D], U8, name=f"e8_{g}") for g in range(G)]
        mu_raw = keep.tile([P, T, L], BF16, name="mu_raw")
        gl_sb = keep.tile([P, T], BF16, name="gl_sb")
        kg_sb = keep.tile([P, G, T], BF16, name="kg_sb")
        t_sb = keep.tile([P, G, T], BF16, name="t_sb")

        def load_pair(dst, view, h):
            nc.sync.dma_start(out=dst[h][:], in_=view[h // 2][:, 2 * (h % 2) : 2 * (h % 2) + 2, :])

        load_pair(u_sb, u_v, 0)
        nc.sync.dma_start(out=e8[0][:], in_=e_v[0])
        load_pair(u_sb, u_v, 1)
        nc.sync.dma_start(out=e8[1][:], in_=e_v[1])
        load_pair(u_sb, u_v, 2)
        load_pair(u_sb, u_v, 3)
        nc.sync.dma_start(out=kg_sb[:], in_=kg.rearrange("b (g p t) -> p (b g) t", g=G, t=T))
        nc.sync.dma_start(out=gl_sb[:], in_=gl.rearrange("(p t) -> p t", t=T))
        nc.sync.dma_start(out=mu_raw[:], in_=mu.rearrange("(p t) n -> p t n", t=T))
        nc.sync.dma_start(out=t_sb[:], in_=t.rearrange("b (g p t) -> p (b g) t", g=G, t=T))
        for h in range(PAIRS):
            load_pair(a_sb, a_v, h)

        ident = keep.tile([P, P], F32, name="ident")
        make_identity(nc, ident[:])
        warm = keep.tile([P, 1], F32, name="warm")
        nc.vector.memset(warm[:], 0.0)
        nc.scalar.activation(out=warm[:], in_=warm[:], func=ACT.Exp)

        neg_max = keep.tile([P, S], F32, name="neg_max")
        ex_sum = keep.tile([P, S], F32, name="ex_sum")
        recip = keep.tile([P, S], F32, name="recip")
        sc_bc = keep.tile([P, D], F32, name="sc_bc")
        e_bf = [keep.tile([P, D], BF16, name=f"ebf{s}") for s in range(S)]
        e_grp = [keep.tile([P, T, P, 4], BF16, name=f"egrp{g}", align_bytes=64) for g in range(G)]
        a_grp = [keep.tile([P, 2, P, 4], BF16, name=f"agrp{h}", align_bytes=64) for h in range(PAIRS)]
        q_grp = [keep.tile([P, T, P, 4], BF16, name=f"qgrp{g}", align_bytes=64) for g in range(G)]
        v_grp = [keep.tile([P, L, 4], BF16, name=f"vgrp{g}", align_bytes=64) for g in range(G)]
        mu_grp = keep.tile([P, L, 4], BF16, name="mu_grp", align_bytes=64)

        def codes(name, width):
            c = keep.tile([P, width], U32, name=name + "_c", align_bytes=64)
            p = keep.tile([P, width], U8, name=name + "_s", align_bytes=64)
            return c, p

        e_q = [codes(f"eq{g}", 512) for g in range(G)]
        a_q = [codes(f"aq{h}", 256) for h in range(PAIRS)]
        q_q = [codes(f"qq{g}", 512) for g in range(G)]
        v_q = [codes(f"vq{g}", 512) for g in range(G)]
        mu_q = codes("muq", 512)

        def quantize(dst, src):
            nc.vector.quantize_mx(out=dst[0][:].bitcast(FP8X4), scales=dst[1][:], in_=src)

        def matmul(o, lhs, lc, rhs, rc, start=True, stop=True):
            nc.tensor.matmul_mx(
                out=o, lhsT=lhs[0][:, lc].bitcast(FP8X4), lhsT_scale=lhs[1][:, lc],
                rhs=rhs[0][:, rc].bitcast(FP8X4), rhs_scale=rhs[1][:, rc], start=start, stop=stop)

        bank_no = [0]

        def bank():
            b = psum.tile([P, 512], F32, name=f"bank{bank_no[0] % 7}")
            bank_no[0] += 1
            return b

        banks = {}
        kg_ps = psum.tile([P, G, T], F32, name="kg_ps")
        ident_bf = keep.tile([P, P], BF16, name="ident_bf")
        make_identity(nc, ident_bf[:])

        def kg_t():
            nc.tensor.matmul(out=kg_ps[:].rearrange("p g t -> p (g t)"), lhsT=ident_bf[:], rhs=kg_sb[:].rearrange("p g t -> p (g t)"), start=True, stop=True)

        def scale_t():
            b = bank()
            for j in range(T):
                nc.tensor.transpose(b[:, j * P : (j + 1) * P], esc[:, j : j + 1].to_broadcast([P, P]), ident[:])
            banks["sc"] = b

        def scale_c():
            nc.scalar.copy(out=sc_bc[:].rearrange("p (q j) -> p q j", j=T), in_=banks["sc"][:].rearrange("p (j q) -> p q j", j=T))

        def e_mul(s):
            nc.vector.tensor_tensor(out=e_bf[s][:], in0=e8[s // T][:, s % T, :].bitcast(FP8), in1=sc_bc[:], op=ALU.mult)

        def word_t(key, srcs):
            b = bank()
            for i, src in enumerate(srcs):
                w = src.bitcast(F32)
                for k in range(2):
                    nc.tensor.transpose(b[:, (2 * i + k) * P : (2 * i + k + 1) * P], w[:, k : 256 : 2], ident[:])
            banks[key] = b

        def word_copy(key, dst):
            nc.scalar.copy(out=dst.bitcast(F32), in_=banks[key][:].rearrange("p (s k r) -> p s r k", s=2, k=2))

        def e_t(h):
            word_t(("e", h), [e_bf[2 * h][:], e_bf[2 * h + 1][:]])

        def e_c(h):
            word_copy(("e", h), e_grp[h // 2][:, 2 * (h % 2) : 2 * (h % 2) + 2, :, :])

        def a_t(h):
            word_t(("a", h), [a_sb[h][:, 0, :], a_sb[h][:, 1, :]])

        def a_c(h):
            word_copy(("a", h), a_grp[h][:])

        def row_max(s):
            dump = work.tile([P, L], BF16, name="dump")
            nc.vector.tensor_scalar(out=dump[:], in0=u_sb[s // 2][:, s % 2, :], scalar1=-1.0, scalar2=None,
                                    op0=ALU.mult, op1=ALU.min, accum_out=neg_max[:, s : s + 1])

        def exp(s):
            x = work.tile([P, T, P], F32, name="ex")
            nc.scalar.activation(out=x[:], in_=u_sb[s // 2][:, s % 2, :].rearrange("m (p t) -> m t p", t=T),
                                 func=ACT.Exp, bias=neg_max[:, s : s + 1], accum_out=ex_sum[:, s : s + 1])
            banks[("ex", s)] = x

        def rec(h):
            nc.vector.reciprocal(out=recip[:, 2 * h : 2 * h + 2], in_=ex_sum[:, 2 * h : 2 * h + 2])

        def z(s, eng):
            zz = work.tile([P, T, P], F32, name="z")
            if eng == "S":
                nc.scalar.activation(out=zz[:], in_=banks[("ex", s)][:], func=ACT.Identity, scale=recip[:, s : s + 1], bias=-1.0 / L)
            elif eng == "V":
                nc.vector.tensor_scalar(out=zz[:], in0=banks[("ex", s)][:], scalar1=recip[:, s : s + 1], scalar2=-1.0 / L, op0=ALU.mult, op1=ALU.add)
            else:
                nc.gpsimd.tensor_scalar(out=zz[:], in0=banks[("ex", s)][:], scalar1=recip[:, s : s + 1], scalar2=-1.0 / L, op0=ALU.mult, op1=ALU.add)
            banks[("z", s)] = zz

        def z_t(s):
            b = bank()
            for j in range(T):
                nc.tensor.transpose(b[:, j * P : (j + 1) * P], banks[("z", s)][:, j, :], ident[:])
            banks[("zt", s)] = b

        def per_word(v):
            return v.unsqueeze(1).to_broadcast([P, P, T])

        def q_mul_s(s):
            for j in range(T):
                nc.scalar.activation(out=q_grp[s // T][:, s % T, :, j], in_=banks[("zt", s)][:, j * P : (j + 1) * P],
                                     func=ACT.Copy, scale=gl_f[:, j : j + 1])

        def v_mul_s(g, lb):
            for j in range(T):
                nc.scalar.activation(out=v_grp[g][:, lb * P : (lb + 1) * P, j], in_=banks[("v", g, lb)][:, j * P : (j + 1) * P],
                                     func=ACT.Copy, scale=t_f[:, g, j : j + 1])

        gl_f = keep.tile([P, T], F32, name="gl_f")
        nc.gpsimd.tensor_copy(out=gl_f[:], in_=gl_sb[:])
        t_f = keep.tile([P, G, T], F32, name="t_f")
        nc.gpsimd.tensor_copy(out=t_f[:], in_=t_sb[:])

        def mu_copy(h, eng):
            c = slice(256 * h, 256 * h + 256)
            dst, src = mu_grp[:, c, :], mu_raw[:, :, c].rearrange("p t n -> p n t")
            if eng == "S":
                nc.scalar.copy(out=dst, in_=src)
            else:
                nc.vector.tensor_copy(out=dst, in_=src)

        def q_mul(s):
            nc.vector.tensor_tensor(out=q_grp[s // T][:, s % T, :, :],
                                    in0=banks[("zt", s)][:].rearrange("p (t m) -> p m t", t=T),
                                    in1=per_word(gl_sb[:]), op=ALU.mult)

        def v_mm(g, lb):
            b = bank()
            for j in range(T):
                matmul(b[:, j * P : (j + 1) * P], q_q[g], slice(j * P, (j + 1) * P), mu_q, slice(lb * P, (lb + 1) * P))
            banks[("v", g, lb)] = b

        def v_mul(g, lb):
            nc.vector.tensor_tensor(out=v_grp[g][:, lb * P : (lb + 1) * P, :],
                                    in0=banks[("v", g, lb)][:].rearrange("p (t m) -> p m t", t=T),
                                    in1=per_word(t_sb[:, g, :]), op=ALU.mult)

        def s_mm(g, ib):
            b = bank()
            c = slice((ib % 2) * P, (ib % 2 + 1) * P)
            for j in range(T):
                matmul(b[:, j * P : (j + 1) * P], e_q[g], slice(j * P, (j + 1) * P), a_q[ib // 2], c)
            banks[("s", g, ib)] = b

        def tanh(g, ib):
            if ("th", ib) not in banks:
                x = work.tile([P, G, P, T], F32, name="th")
                banks[("th", ib)] = x
            nc.scalar.activation(out=banks[("th", ib)][:, g, :, :], in_=banks[("s", g, ib)][:].rearrange("p (t m) -> p m t", t=T),
                                 func=ACT.Tanh, scale=D ** -0.5)

        def kk(ib):
            if ("kk", ib) not in banks:
                x = work.tile([P, G, P, T], BF16, name="kk", align_bytes=64)
                banks[("kk", ib)] = x
            return banks[("kk", ib)]

        def k_mul(g, ib):
            nc.vector.tensor_tensor(out=kk(ib)[:, g, :, :], in0=banks[("th", ib)][:, g, :, :],
                                    in1=per_word(kg_ps[:, g, :]), op=ALU.mult)

        def k_mul_g(g, ib):
            nc.gpsimd.tensor_tensor(out=kk(ib)[:, g, :, :], in0=banks[("th", ib)][:, g, :, :],
                                    in1=per_word(kg_sb[:, g, :]), op=ALU.mult)

        def k_quant(ib):
            c = work.tile([P, G * P], U32, name="kc", align_bytes=64)
            p = work.tile([P, G * P], U8, name="ks", align_bytes=64)
            banks[("kq", ib)] = (c, p)
            quantize((c, p), banks[("kk", ib)][:].rearrange("p g m t -> p (g m t)"))

        def o_mm(ib):
            b = bank()
            for g in range(G):
                matmul(b[:], banks[("kq", ib)], slice(g * P, (g + 1) * P), v_q[g], slice(0, L), start=(g == 0), stop=(g == G - 1))
            banks[("o", ib)] = b

        def finish(ib):
            o = work.tile([P, L], F32, name="o")
            nc.vector.scalar_tensor_tensor(out=o[:], in0=banks[("o", ib)][:], scalar=-float(L) * N ** -0.5,
                                           in1=u_sb[ib // 2][:, ib % 2, :], op0=ALU.mult, op1=ALU.add)
            nc.sync.dma_start(out=out_v[ib // T][:, ib % T, :], in_=o[:])

        def each(f, *xs):
            for x in xs:
                f(x)

        row_max(0)
        scale_t()
        row_max(1)
        scale_c()
        exp(0)
        e_mul(1)
        e_mul(0)
        e_t(0)
        exp(1)
        row_max(2)
        rec(0)
        e_mul(7)
        e_mul(6)
        z(1, "S")
        z_t(1)
        z(0, "S")
        exp(2)
        e_t(3)
        row_max(6)
        a_t(0)
        a_t(2)
        e_c(0)
        row_max(7)
        row_max(3)
        exp(7)
        mu_copy(0, "V")
        exp(3)
        e_mul(4)
        e_c(3)
        e_mul(5)
        e_mul(3)
        e_t(2)
        exp(6)
        rec(1)
        z(2, "S")
        e_mul(2)
        z_t(2)
        mu_copy(1, "V")
        a_c(2)
        z(3, "G")
        row_max(4)
        a_t(1)
        e_t(1)
        q_mul(1)
        e_c(2)
        rec(3)
        a_c(0)
        exp(4)
        z_t(3)
        quantize(e_q[1], e_grp[1][:].rearrange("p t m w -> p (t m w)"))
        a_c(1)
        row_max(5)
        e_c(1)
        z_t(0)
        q_mul(2)
        exp(5)
        quantize(a_q[0], a_grp[0][:].rearrange("p t m w -> p (t m w)"))
        quantize(a_q[1], a_grp[1][:].rearrange("p t m w -> p (t m w)"))
        quantize(a_q[2], a_grp[2][:].rearrange("p t m w -> p (t m w)"))
        quantize(e_q[0], e_grp[0][:].rearrange("p t m w -> p (t m w)"))
        rec(2)
        z(6, "S")
        q_mul(0)
        q_mul(3)
        s_mm(1, 4)
        s_mm(0, 0)
        z(4, "S")
        s_mm(1, 0)
        quantize(mu_q, mu_grp[:].rearrange("p n t -> p (n t)"))
        s_mm(0, 1)
        tanh(1, 4)
        z_t(4)
        z_t(6)
        quantize(q_q[0], q_grp[0][:].rearrange("p t m w -> p (t m w)"))
        kg_t()
        tanh(0, 0)
        tanh(1, 0)
        s_mm(1, 2)
        k_mul(1, 4)
        z(5, "S")
        z(7, "G")
        tanh(0, 1)
        s_mm(1, 1)
        tanh(1, 2)
        q_mul(6)
        z_t(5)
        a_t(3)
        tanh(1, 1)
        z_t(7)
        s_mm(0, 2)
        s_mm(0, 5)
        s_mm(1, 3)
        a_c(3)
        tanh(0, 2)
        v_mm(0, 3)
        k_mul_g(0, 0)
        q_mul(4)
        tanh(0, 5)
        tanh(1, 3)
        s_mm(1, 5)
        s_mm(0, 4)
        tanh(1, 5)
        s_mm(0, 3)
        k_mul(1, 0)
        q_mul(5)
        q_mul(7)
        quantize(a_q[3], a_grp[3][:].rearrange("p t m w -> p (t m w)"))
        tanh(0, 4)
        v_mm(0, 1)
        k_quant(0)
        quantize(q_q[1], q_grp[1][:].rearrange("p t m w -> p (t m w)"))
        v_mul(0, 3)
        v_mm(1, 3)
        k_mul_g(0, 1)
        k_mul(0, 5)
        v_mm(1, 1)
        v_mm(1, 0)
        v_mm(0, 0)
        v_mm(0, 2)
        tanh(0, 3)
        k_mul(1, 1)
        v_mul(0, 1)
        s_mm(0, 7)
        k_mul_g(0, 2)
        v_mul(1, 0)
        v_mm(1, 2)
        k_mul(1, 3)
        k_mul_g(0, 4)
        s_mm(0, 6)
        v_mul(0, 2)
        k_mul(1, 5)
        v_mul(0, 0)
        v_mul_s(1, 1)
        k_mul(0, 3)
        v_mul_s(1, 3)
        k_quant(5)
        k_quant(3)
        v_mul_s(1, 2)
        k_mul_g(1, 2)
        k_quant(2)
        tanh(0, 6)
        quantize(v_q[0], v_grp[0][:].rearrange("p n t -> p (n t)"))
        k_quant(1)
        s_mm(1, 7)
        quantize(v_q[1], v_grp[1][:].rearrange("p n t -> p (n t)"))
        s_mm(1, 6)
        o_mm(2)
        tanh(0, 7)
        k_quant(4)
        tanh(1, 7)
        o_mm(1)
        o_mm(5)
        tanh(1, 6)
        o_mm(3)
        k_mul(0, 7)
        k_mul(1, 7)
        finish(2)
        o_mm(4)
        k_mul_g(0, 6)
        o_mm(0)
        finish(1)
        k_mul_g(1, 6)
        finish(5)
        finish(3)
        k_quant(7)
        finish(4)
        o_mm(7)
        k_quant(6)
        o_mm(6)
        finish(0)
        finish(7)
        finish(6)
